import numpy as np
import ml_dtypes


def mxq(x, axis, fmt="e4m3"):
    dtype, down = {"e4m3": (ml_dtypes.float8_e4m3fn, 7), "e5m2": (ml_dtypes.float8_e5m2, 14)}[fmt]
    v = np.moveaxis(np.asarray(x, np.float32).astype(ml_dtypes.bfloat16).astype(np.float64), axis, -1)
    blocks = v.reshape(v.shape[:-1] + (-1, 32))
    amax = np.abs(blocks).max(-1, keepdims=True)
    byte = np.maximum(np.where(amax > 0, np.frexp(amax)[1] - 1 + 127, 0) - down, 1)
    scale = np.exp2(byte - 127.0)
    codes = (blocks / scale).astype(np.float32).astype(dtype).astype(np.float64)
    return np.moveaxis((codes * scale).reshape(v.shape), -1, axis)


WIDE = False


def mx_kscale(k):
    if not WIDE:
        return np.ones(k)
    levels = np.array([10, -10, 5, -5, 0])
    if k % 512:
        return np.exp2(np.random.permutation(np.resize(levels, k // 32))).repeat(32)
    a = np.empty((k // 512, 16))
    for p in range(k // 512):
        a[p, :8] = np.random.permutation(np.resize(levels, 8))
        for g in range(8):
            far = levels[np.abs(levels - a[p, g]) >= 10]
            a[p, g + 8] = far[np.random.randint(len(far))]
    return np.exp2(a.ravel()).repeat(32)


def f64(x):
    return np.asarray(x).astype(np.float64)


def striped(idx):
    return np.tile(idx.reshape(-1, 16).T, (8, 1)).astype(np.uint16)


def unstriped(offs):
    return offs[:16].T.reshape(-1).astype(np.int64)


def striped8(idx):
    return np.concatenate([x.reshape(-1, 16).T for x in idx]).astype(np.uint16)


def runs(offs, k):
    lists = np.stack([offs[16 * r : 16 * r + 16].T.reshape(-1) for r in range(8)]).astype(np.int64)
    return lists[np.arange(k) % 512 // 64]


def pack_weight(w):
    k, n = w.shape
    w = f64(np.asarray(w, np.float32).astype(ml_dtypes.bfloat16)).reshape(k // 32, 32, n)
    amax = np.abs(w).max(1)
    byte = np.clip(np.where(amax > 0, np.frexp(amax)[1] - 1 + 127 - 7, 1), 1, 254)
    scaled = (w * np.exp2(127.0 - byte)[:, None, :]).reshape(k, n).astype(np.float32)
    words = np.ascontiguousarray(scaled.reshape(k // 512, 128, 4, n).transpose(0, 1, 3, 2)).astype(ml_dtypes.float8_e4m3fn).view(np.uint8)
    return words, np.ascontiguousarray(byte.astype(np.uint8).reshape(k // 512, 16, n))


def unpack_weight(words, scales):
    g, p, n, _ = words.shape
    vals = np.ascontiguousarray(words).view(ml_dtypes.float8_e4m3fn).astype(np.float64) * np.repeat(np.exp2(scales.astype(np.float64) - 127.0), 8, axis=1)[..., None]
    return vals.transpose(0, 1, 3, 2).reshape(g * 512, n)


def relu(v):
    return np.maximum(v, 0.0)

def planes(y):
    n, m = y.shape
    v = y.astype(np.float32).astype(ml_dtypes.bfloat16).astype(np.float64).reshape(n // 32, 32, m)
    top = np.abs(v).max(1)
    byte = np.clip(np.where(top > 0, np.frexp(top)[1] - 1 + 127 - 7, 1), 1, 254)
    codes = (v * np.exp2(127.0 - byte)[:, None, :]).reshape(n, m).astype(np.float32).astype(ml_dtypes.float8_e4m3fn).view(np.uint8)
    words = codes.reshape(n // 512, 128, 4, m).transpose(0, 1, 3, 2)
    return np.ascontiguousarray(words), np.ascontiguousarray(byte.astype(np.uint8).reshape(n // 512, 16, m))


K, T, S, G, H, U, C = 512, 1024, 512, 2048, 512, 1024, 512


def setup_inputs():
    n = np.random.standard_normal
    s = mx_kscale(K)[:, None]
    packed_xT = pack_weight(n((K, T)) * s)
    packed_dT = pack_weight(n((K, G)) / s)
    return {
        "x_words": packed_xT[0],
        "x_scales": packed_xT[1],
        "d_words": packed_dT[0],
        "d_scales": packed_dT[1],
        "gs": (np.random.uniform(0.5, 1.5, (K, 1)) / s).astype(np.float32),
        "offs": striped(np.random.permutation(T)[:S]),
        "k1": striped8(np.random.randint(0, G, (8, H))),
        "n1": striped8(np.stack([np.random.permutation(U)[:S] for _ in range(8)])),
        "n2": striped8(np.stack([np.random.permutation(S) for _ in range(8)])),
        "cand": striped(np.random.permutation(T)[:C]),
        "n3": striped8(np.stack([np.random.permutation(U) for _ in range(8)])),
        "n4": striped8(np.stack([np.random.permutation(U) for _ in range(8)])),
    }


def reference(x_words, x_scales, d_words, d_scales, gs, offs, k1, n1, n2, cand, n3, n4):
    x_cand = unpack_weight(x_words, x_scales)[:, unstriped(cand)]
    d_k1 = unpack_weight(d_words, d_scales)[np.arange(K)[:, None], runs(k1, K)]
    xq = unpack_weight(x_words, x_scales)[:, unstriped(offs)]
    h = 0.0625 * (d_k1.T @ xq)
    nw = h - (relu(h[np.arange(H)[:, None], runs(n2, H)]))
    pg = np.zeros((H, U))
    pg[np.arange(H)[:, None], runs(n1, H)] = nw
    z = f64(gs) * pg
    s = 0.0625 * ((x_cand.T @ mxq(z, 0, "e4m3")))
    st = np.maximum(s, s[np.arange(C)[:, None], runs(n3, C)])
    out_0 = st[np.arange(C)[:, None], runs(n4, C)] - (0.5 * s)
    return (out_0,) + planes(out_0)

@@ -1,0 +1,231 @@
+from contextlib import ExitStack
+
+import concourse.mybir as mybir
+
+K, T, S, G, H, U, C = 512, 1024, 512, 2048, 512, 1024, 512
+FLOPS = 2 * K * H * S + 2 * H * C * U
+
+F32 = mybir.dt.float32
+BF16 = mybir.dt.bfloat16
+I32 = mybir.dt.int32
+U32 = mybir.dt.uint32
+U16 = mybir.dt.uint16
+U8 = mybir.dt.uint8
+FP8X4 = mybir.dt.float8_e4m3fn_x4
+ADD = mybir.AluOpType.add
+MAX = mybir.AluOpType.max
+COPY = mybir.ActivationFunctionType.Copy
+RELU = mybir.ActivationFunctionType.Relu
+
+P = 128
+PACK = 4
+STRIPE = 16
+Z_PIECES = ((0, 512), (512, 256), (768, 256))
+OUT_PIECES = ((0, 512), (512, 256), (768, 256))
+
+
+def tile_picked_pqcpagezhopb_none_po_kernel(
+    tc, x_words, x_scales, d_words, d_scales, gs, offs, k1, n1, n2, cand, n3, n4, out_0, out_1, out_2
+):
+    nc = tc.nc
+
+    with ExitStack() as ctx:
+        lists = ctx.enter_context(tc.tile_pool(name="lists", bufs=1))
+        keep = ctx.enter_context(tc.tile_pool(name="keep", bufs=1))
+        ring = ctx.enter_context(tc.tile_pool(name="ring", bufs=2))
+        psum = ctx.enter_context(tc.psum_pool(name="psum", bufs=1))
+
+        def load_list(src, name):
+            held = lists.tile(list(src.shape), U16, name=name)
+            nc.sync.dma_start(held[:], src)
+            return held
+
+        def entries(held, first, count):
+            return held[:, first // STRIPE : (first + count) // STRIPE]
+
+        def words_of(planes):
+            return planes[0].rearrange("p n t -> p (n t)").bitcast(I32)
+
+        def deal(dst, src):
+            nc.vector.tensor_copy(dst.rearrange("p (t m) -> p t m", t=PACK), src.rearrange("p (m t) -> p t m", t=PACK))
+
+        d_scale_table = keep.tile([P, G], U8, align_bytes=64)
+        x_scale_table = keep.tile([P, T], U8, align_bytes=64)
+        nc.gpsimd.memset(d_scale_table[:].bitcast(I32), 0)
+        nc.vector.memset(x_scale_table[:].bitcast(I32), 0)
+
+        k1_sb = load_list(k1, "k1_sb")
+        x_table = keep.tile([P, T], U32, align_bytes=64)
+        nc.sync.dma_start(x_table[:].bitcast(I32), words_of(x_words))
+        nc.sync.dma_start(d_scale_table[0:P:8, :].bitcast(I32), d_scales[0].bitcast(I32))
+        offs_sb = load_list(offs, "offs_sb")
+        d_table = keep.tile([P, G], U32, align_bytes=64)
+        nc.sync.dma_start(d_table[:].bitcast(I32), words_of(d_words))
+        for j in range(4):
+            nc.sync.dma_start(x_scale_table[j:P:32, :].bitcast(I32), x_scales[0][j:16:4, :].bitcast(I32))
+        gain = keep.tile([P, PACK], F32)
+        nc.gpsimd.dma_start(gain[:], gs.rearrange("(p t) o -> p (t o)", t=PACK))
+        n2_sb = load_list(n2, "n2_sb")
+        n1_sb = load_list(n1, "n1_sb")
+        cand_sb = load_list(cand, "cand_sb")
+        n3_sb = load_list(n3, "n3_sb")
+        n4_sb = load_list(n4, "n4_sb")
+
+        pages = [keep.tile([P, U], F32, name=f"page{t}") for t in range(PACK)]
+        for t in range(PACK):
+            (nc.vector if t < 3 else nc.gpsimd).memset(pages[t][:], 0.0)
+
+        gain_pos = keep.tile([P, PACK], F32)
+        gain_neg = keep.tile([P, PACK], F32)
+        nc.scalar.activation(gain_pos[:], gain[:], COPY, scale=0.0625)
+        nc.scalar.activation(gain_neg[:], gain[:], COPY, scale=-0.0625)
+
+        d_scale_picked = keep.tile([P, H], U8, align_bytes=64)
+        nc.vector.tensor_copy(d_scale_picked[:], d_scale_table[:].indirect(k1_sb[:]))
+        d_scale_placed = keep.tile([P, H], U8, align_bytes=64)
+        deal(d_scale_placed[:], d_scale_picked[:])
+        for j in range(1, 4):
+            nc.scalar.dma_start(d_scale_placed[j:P:32, :].bitcast(I32), d_scale_placed[8 * j : P : 32, :].bitcast(I32))
+
+        xq_words = keep.tile([P, S], U32, align_bytes=64)
+        nc.vector.tensor_copy(xq_words[:], x_table[:].indirect(offs_sb[:]))
+        xq_scales = keep.tile([P, S], U8, align_bytes=64)
+        nc.vector.tensor_copy(xq_scales[:], x_scale_table[:].indirect(offs_sb[:]))
+        d_picked = keep.tile([P, H], U32, align_bytes=64)
+        nc.vector.tensor_copy(d_picked[:], d_table[:].indirect(k1_sb[:]))
+        d_dealt = keep.tile([P, H], U32, align_bytes=64)
+        deal(d_dealt[:].bitcast(I32), d_picked[:].bitcast(I32))
+
+        cut, whole = [], []
+        for t in range(PACK):
+            rows = slice(t * P, (t + 1) * P)
+            h_sum = psum.tile([P, S], F32, name=f"h_sum{t}", tag=f"bank{t}")
+            nc.tensor.matmul_mx(
+                out=h_sum[:],
+                lhsT=d_dealt[:, rows].bitcast(FP8X4),
+                lhsT_scale=d_scale_placed[:, rows],
+                rhs=xq_words[:].bitcast(FP8X4),
+                rhs_scale=xq_scales[:],
+                start=True,
+                stop=True,
+            )
+            positive = ring.tile([P, S], F32, name="positive")
+            nc.scalar.activation(positive[:], h_sum[:], RELU)
+            cut.append(keep.tile([P, S], F32, name=f"cut{t}"))
+            nc.scalar.activation(cut[t][:], positive[:], COPY, scale=gain_neg[:, t : t + 1])
+            whole.append(keep.tile([P, S], F32, name=f"whole{t}"))
+            nc.scalar.activation(whole[t][:], h_sum[:], COPY, scale=gain_pos[:, t : t + 1])
+
+        c_picked = keep.tile([P, C], U32, align_bytes=64)
+        nc.vector.tensor_copy(c_picked[:], x_table[:].indirect(cand_sb[:]))
+        c_dealt = keep.tile([P, C], U32, align_bytes=64)
+        deal(c_dealt[:].bitcast(I32), c_picked[:].bitcast(I32))
+
+        z_round = [keep.tile([P, w, PACK], BF16, name=f"z_round{i}", align_bytes=64) for i, (c0, w) in enumerate(Z_PIECES)]
+        fetched = [keep.tile([P, S], F32, name=f"fetched{t}") for t in range(PACK)]
+
+        def fetch_cut(t):
+            for first in range(0, S, S // 2):
+                nc.vector.tensor_copy(
+                    fetched[t][:, first : first + S // 2], cut[t][:].indirect(entries(n2_sb, first, S // 2))
+                )
+
+        fetch_cut(0)
+        for t in range(PACK):
+            if t + 1 < PACK:
+                fetch_cut(t + 1)
+            nc.vector.tensor_tensor(pages[t][:].indirect(n1_sb[:]), fetched[t][:], whole[t][:], ADD)
+            for i, (first, w) in enumerate(Z_PIECES):
+                nc.scalar.copy(z_round[i][:, :, t], pages[t][:, first : first + w])
+
+        c_scale_picked = keep.tile([P, C], U8, align_bytes=64)
+        nc.vector.tensor_copy(c_scale_picked[:], x_scale_table[:].indirect(cand_sb[:]))
+        c_scale_dealt = keep.tile([P, C], U8, align_bytes=64)
+        deal(c_scale_dealt[:], c_scale_picked[:])
+
+        z_words, z_scales = [], []
+        for i, (first, w) in enumerate(Z_PIECES):
+            z_words.append(keep.tile([P, w], U32, name=f"z_words{i}", align_bytes=64))
+            z_scales.append(keep.tile([P, w], U8, name=f"z_scales{i}", align_bytes=64))
+            nc.vector.quantize_mx(
+                out=z_words[i][:].bitcast(FP8X4),
+                scales=z_scales[i][:],
+                in_=z_round[i][:].rearrange("p w t -> p (w t)"),
+            )
+
+        banks = [psum.tile([P, 512], F32, name=f"s_sum{b}", tag=f"bank{b}") for b in range(8)]
+
+        def s_sum(t, i):
+            w = Z_PIECES[i][1]
+            if i == 0:
+                return banks[t][:]
+            return banks[2 + 2 * i + min(t, 3 - t)][:, (t // 2) * w : (t // 2 + 1) * w]
+
+        score = [keep.tile([P, U], F32, name=f"score{t}") for t in range(PACK)]
+        less_half = [keep.tile([P, U], F32, name=f"less_half{t}") for t in range(PACK)]
+        best = [keep.tile([P, U], F32, name=f"best{t}") for t in range(PACK)]
+        other = [keep.tile([P, U], F32, name=f"other{t}") for t in range(PACK)]
+        for t in range(PACK):
+            rows = slice(t * P, (t + 1) * P)
+            for i, (first, w) in enumerate(Z_PIECES):
+                nc.tensor.matmul_mx(
+                    out=s_sum(t, i),
+                    lhsT=c_dealt[:, rows].bitcast(FP8X4),
+                    lhsT_scale=c_scale_dealt[:, rows],
+                    rhs=z_words[i][:].bitcast(FP8X4),
+                    rhs_scale=z_scales[i][:],
+                    start=True,
+                    stop=True,
+                )
+                nc.scalar.activation(score[t][:, first : first + w], s_sum(t, i), COPY, scale=0.0625)
+        for t in range(PACK):
+            for i, (first, w) in enumerate(Z_PIECES):
+                nc.scalar.activation(less_half[t][:, first : first + w], s_sum(t, i), COPY, scale=-0.03125)
+
+        def fetch_other(t):
+            for first in range(0, U, U // 2):
+                nc.vector.tensor_copy(
+                    other[t][:, first : first + U // 2], score[t][:].indirect(entries(n3_sb, first, U // 2))
+                )
+
+        fetch_other(0)
+        for t in range(PACK):
+            if t + 1 < PACK:
+                fetch_other(t + 1)
+            nc.vector.tensor_tensor(best[t][:], other[t][:], score[t][:], MAX)
+
+        out_rows = out_0.rearrange("(p t) w -> p t w", t=PACK)
+        out_words = words_of(out_1)
+        y_scales = keep.tile([P, U], U8, align_bytes=64)
+        rounded = []
+
+        def finish(i):
+            first, w = OUT_PIECES[i]
+            y_words = keep.tile([P, w], U32, name=f"y_words{i}", align_bytes=64)
+            nc.vector.quantize_mx(
+                out=y_words[:].bitcast(FP8X4),
+                scales=y_scales[:, first : first + w],
+                in_=rounded[i][:].rearrange("p w t -> p (w t)"),
+            )
+            nc.sync.dma_start(out_words[:, first : first + w], y_words[:].bitcast(I32))
+
+        for i, (first, w) in enumerate(OUT_PIECES):
+            y = keep.tile([P, PACK, w], F32, name=f"y{i}")
+            for t in range(PACK):
+                nc.vector.tensor_tensor(
+                    y[:, t, :],
+                    best[t][:].indirect(entries(n4_sb, first, w)),
+                    less_half[t][:, first : first + w],
+                    ADD,
+                )
+            nc.sync.dma_start(out_rows[:, :, first : first + w], y[:])
+            rounded.append(keep.tile([P, w, PACK], BF16, name=f"y_round{i}", align_bytes=64))
+            if i + 1 < len(OUT_PIECES):
+                nc.scalar.copy(rounded[i][:], y[:].rearrange("p t w -> p w t"))
+            else:
+                nc.vector.tensor_copy(rounded[i][:], y[:].rearrange("p t w -> p w t"))
+            if i > 0:
+                finish(i - 1)
+        finish(len(OUT_PIECES) - 1)
+        for j in range(4):
+            nc.scalar.dma_start(out_2[0][j:16:4, :].bitcast(I32), y_scales[j:P:32, :].bitcast(I32))

@@ -14,13 +14,15 @@ U8 = mybir.dt.uint8
 FP8X4 = mybir.dt.float8_e4m3fn_x4
 ADD = mybir.AluOpType.add
 MAX = mybir.AluOpType.max
+MULT = mybir.AluOpType.mult
+SUB = mybir.AluOpType.subtract
 COPY = mybir.ActivationFunctionType.Copy
 RELU = mybir.ActivationFunctionType.Relu
 
 P = 128
 PACK = 4
 STRIPE = 16
-Z_PIECES = ((0, 512), (512, 256), (768, 256))
+Z_PIECES = ((0, 256), (256, 256), (512, 256), (768, 256))
 OUT_PIECES = ((0, 512), (512, 256), (768, 256))
 
 
@@ -51,29 +53,30 @@ def tile_picked_pqcpagezhopb_none_po_kernel(
 
         d_scale_table = keep.tile([P, G], U8, align_bytes=64)
         x_scale_table = keep.tile([P, T], U8, align_bytes=64)
-        nc.gpsimd.memset(d_scale_table[:].bitcast(I32), 0)
-        nc.vector.memset(x_scale_table[:].bitcast(I32), 0)
+        nc.gpsimd.memset(d_scale_table[:, : G // 2].bitcast(I32), 0)
+        nc.vector.memset(d_scale_table[:, G // 2 :].bitcast(I32), 0)
+        nc.gpsimd.memset(x_scale_table[:].bitcast(I32), 0)
 
         k1_sb = load_list(k1, "k1_sb")
         x_table = keep.tile([P, T], U32, align_bytes=64)
         nc.sync.dma_start(x_table[:].bitcast(I32), words_of(x_words))
-        nc.sync.dma_start(d_scale_table[0:P:8, :].bitcast(I32), d_scales[0].bitcast(I32))
+        nc.scalar.dma_start(d_scale_table[0:P:8, :].bitcast(I32), d_scales[0].bitcast(I32))
         offs_sb = load_list(offs, "offs_sb")
+        n2_sb = load_list(n2, "n2_sb")
+        n1_sb = load_list(n1, "n1_sb")
         d_table = keep.tile([P, G], U32, align_bytes=64)
         nc.sync.dma_start(d_table[:].bitcast(I32), words_of(d_words))
         for j in range(4):
             nc.sync.dma_start(x_scale_table[j:P:32, :].bitcast(I32), x_scales[0][j:16:4, :].bitcast(I32))
         gain = keep.tile([P, PACK], F32)
         nc.gpsimd.dma_start(gain[:], gs.rearrange("(p t) o -> p (t o)", t=PACK))
-        n2_sb = load_list(n2, "n2_sb")
-        n1_sb = load_list(n1, "n1_sb")
         cand_sb = load_list(cand, "cand_sb")
         n3_sb = load_list(n3, "n3_sb")
         n4_sb = load_list(n4, "n4_sb")
 
         pages = [keep.tile([P, U], F32, name=f"page{t}") for t in range(PACK)]
         for t in range(PACK):
-            (nc.vector if t < 3 else nc.gpsimd).memset(pages[t][:], 0.0)
+            (nc.vector if t < 2 else nc.gpsimd).memset(pages[t][:].bitcast(I32), 0)
 
         gain_pos = keep.tile([P, PACK], F32)
         gain_neg = keep.tile([P, PACK], F32)
@@ -91,7 +94,7 @@ def tile_picked_pqcpagezhopb_none_po_kernel(
         nc.vector.tensor_copy(xq_words[:], x_table[:].indirect(offs_sb[:]))
         xq_scales = keep.tile([P, S], U8, align_bytes=64)
         nc.vector.tensor_copy(xq_scales[:], x_scale_table[:].indirect(offs_sb[:]))
-        d_picked = keep.tile([P, H], U32, align_bytes=64)
+        d_picked = keep.tile([P, H], U32, align_bytes=64, tag="picked")
         nc.vector.tensor_copy(d_picked[:], d_table[:].indirect(k1_sb[:]))
         d_dealt = keep.tile([P, H], U32, align_bytes=64)
         deal(d_dealt[:].bitcast(I32), d_picked[:].bitcast(I32))
@@ -111,42 +114,53 @@ def tile_picked_pqcpagezhopb_none_po_kernel(
             )
             positive = ring.tile([P, S], F32, name="positive")
             nc.scalar.activation(positive[:], h_sum[:], RELU)
-            cut.append(keep.tile([P, S], F32, name=f"cut{t}"))
-            nc.scalar.activation(cut[t][:], positive[:], COPY, scale=gain_neg[:, t : t + 1])
-            whole.append(keep.tile([P, S], F32, name=f"whole{t}"))
-            nc.scalar.activation(whole[t][:], h_sum[:], COPY, scale=gain_pos[:, t : t + 1])
+            if t == 0:
+                cut.append(keep.tile([P, S], F32, name="cut0"))
+                whole0 = keep.tile([P, S], F32)
+                whole.append(whole0[:])
+            else:
+                cut.append(keep.tile([P, 2 * S], F32, name=f"cut{t}"))
+                whole.append(cut[t][:, S:])
+            nc.scalar.activation(cut[t][:, :S], positive[:], COPY, scale=gain_neg[:, t : t + 1])
+            nc.scalar.activation(whole[t], h_sum[:], COPY, scale=gain_pos[:, t : t + 1])
 
-        c_picked = keep.tile([P, C], U32, align_bytes=64)
+        c_picked = keep.tile([P, C], U32, align_bytes=64, tag="picked")
         nc.vector.tensor_copy(c_picked[:], x_table[:].indirect(cand_sb[:]))
         c_dealt = keep.tile([P, C], U32, align_bytes=64)
         deal(c_dealt[:].bitcast(I32), c_picked[:].bitcast(I32))
+
+        c_scale_picked = keep.tile([P, C], U8, align_bytes=64, tag="picked")
+        nc.vector.tensor_copy(c_scale_picked[:], x_scale_table[:].indirect(cand_sb[:]))
+        c_scale_dealt = keep.tile([P, C], U8, align_bytes=64)
+        deal(c_scale_dealt[:], c_scale_picked[:])
 
         z_round = [keep.tile([P, w, PACK], BF16, name=f"z_round{i}", align_bytes=64) for i, (c0, w) in enumerate(Z_PIECES)]
         fetched = [keep.tile([P, S], F32, name=f"fetched{t}") for t in range(PACK)]
 
         def fetch_cut(t):
-            for first in range(0, S, S // 2):
-                nc.vector.tensor_copy(
-                    fetched[t][:, first : first + S // 2], cut[t][:].indirect(entries(n2_sb, first, S // 2))
-                )
+            count = cut[t].shape[1] // 2
+            for first in range(0, S, count):
+                nc.vector.tensor_copy(fetched[t][:, first : first + count], cut[t][:].indirect(entries(n2_sb, first, count)))
 
         fetch_cut(0)
         for t in range(PACK):
             if t + 1 < PACK:
                 fetch_cut(t + 1)
-            nc.vector.tensor_tensor(pages[t][:].indirect(n1_sb[:]), fetched[t][:], whole[t][:], ADD)
+            nc.vector.tensor_tensor(pages[t][:].indirect(n1_sb[:]), fetched[t][:], whole[t], ADD)
             for i, (first, w) in enumerate(Z_PIECES):
-                nc.scalar.copy(z_round[i][:, :, t], pages[t][:, first : first + w])
+                if t == PACK - 1 and i < 2:
+                    nc.vector.tensor_copy(z_round[i][:, :, t], pages[t][:, first : first + w])
+                elif t == PACK - 2 and i < 2:
+                    both = pages[t][:, first : first + w].unsqueeze(2).to_broadcast([P, w, 2])
+                    nc.scalar.copy(z_round[i][:, :, t:], both)
+                else:
+                    nc.scalar.copy(z_round[i][:, :, t], pages[t][:, first : first + w])
 
-        c_scale_picked = keep.tile([P, C], U8, align_bytes=64)
-        nc.vector.tensor_copy(c_scale_picked[:], x_scale_table[:].indirect(cand_sb[:]))
-        c_scale_dealt = keep.tile([P, C], U8, align_bytes=64)
-        deal(c_scale_dealt[:], c_scale_picked[:])
-
-        z_words, z_scales = [], []
-        for i, (first, w) in enumerate(Z_PIECES):
-            z_words.append(keep.tile([P, w], U32, name=f"z_words{i}", align_bytes=64))
-            z_scales.append(keep.tile([P, w], U8, name=f"z_scales{i}", align_bytes=64))
+        z_words, z_scales = {}, {}
+        for i in (2, 0, 1, 3):
+            w = Z_PIECES[i][1]
+            z_words[i] = keep.tile([P, w], U32, name=f"z_words{i}", align_bytes=64)
+            z_scales[i] = keep.tile([P, w], U8, name=f"z_scales{i}", align_bytes=64)
             nc.vector.quantize_mx(
                 out=z_words[i][:].bitcast(FP8X4),
                 scales=z_scales[i][:],
@@ -155,32 +169,42 @@ def tile_picked_pqcpagezhopb_none_po_kernel(
 
         banks = [psum.tile([P, 512], F32, name=f"s_sum{b}", tag=f"bank{b}") for b in range(8)]
 
-        def s_sum(t, i):
-            w = Z_PIECES[i][1]
-            if i == 0:
-                return banks[t][:]
-            return banks[2 + 2 * i + min(t, 3 - t)][:, (t // 2) * w : (t // 2 + 1) * w]
+        def s_sum(t, first, w):
+            if t in (0, 3):
+                return banks[first // 256][:, (t // 3) * 256 : (t // 3) * 256 + w]
+            return banks[2 + 2 * t + first // 512][:, first % 512 : first % 512 + w]
+
+        def runs(t):
+            w = 256 if t in (0, 3) else 512
+            return [(first, w) for first in range(0, U, w)]
 
         score = [keep.tile([P, U], F32, name=f"score{t}") for t in range(PACK)]
         less_half = [keep.tile([P, U], F32, name=f"less_half{t}") for t in range(PACK)]
         best = [keep.tile([P, U], F32, name=f"best{t}") for t in range(PACK)]
         other = [keep.tile([P, U], F32, name=f"other{t}") for t in range(PACK)]
-        for t in range(PACK):
+
+        def multiply(t, i):
+            first, w = Z_PIECES[i]
             rows = slice(t * P, (t + 1) * P)
-            for i, (first, w) in enumerate(Z_PIECES):
-                nc.tensor.matmul_mx(
-                    out=s_sum(t, i),
-                    lhsT=c_dealt[:, rows].bitcast(FP8X4),
-                    lhsT_scale=c_scale_dealt[:, rows],
-                    rhs=z_words[i][:].bitcast(FP8X4),
-                    rhs_scale=z_scales[i][:],
-                    start=True,
-                    stop=True,
-                )
-                nc.scalar.activation(score[t][:, first : first + w], s_sum(t, i), COPY, scale=0.0625)
-        for t in range(PACK):
-            for i, (first, w) in enumerate(Z_PIECES):
-                nc.scalar.activation(less_half[t][:, first : first + w], s_sum(t, i), COPY, scale=-0.03125)
+            nc.tensor.matmul_mx(
+                out=s_sum(t, first, w),
+                lhsT=c_dealt[:, rows].bitcast(FP8X4),
+                lhsT_scale=c_scale_dealt[:, rows],
+                rhs=z_words[i][:].bitcast(FP8X4),
+                rhs_scale=z_scales[i][:],
+                start=True,
+                stop=True,
+            )
+
+        for i in (2, 0, 1, 3):
+            multiply(0, i)
+            first, w = Z_PIECES[i]
+            nc.scalar.activation(score[0][:, first : first + w], s_sum(0, first, w), COPY, scale=0.0625)
+        for t in range(1, PACK):
+            for i in range(len(Z_PIECES)):
+                multiply(t, i)
+            for first, w in runs(t):
+                nc.scalar.activation(score[t][:, first : first + w], s_sum(t, first, w), COPY, scale=0.0625)
 
         def fetch_other(t):
             for first in range(0, U, U // 2):
@@ -188,11 +212,23 @@ def tile_picked_pqcpagezhopb_none_po_kernel(
                     other[t][:, first : first + U // 2], score[t][:].indirect(entries(n3_sb, first, U // 2))
                 )
 
-        fetch_other(0)
         for t in range(PACK):
-            if t + 1 < PACK:
-                fetch_other(t + 1)
-            nc.vector.tensor_tensor(best[t][:], other[t][:], score[t][:], MAX)
+            fetch_other(t)
+            if t < 2:
+                gap = keep.tile([P, U], F32, name=f"gap{t}")
+                lift = keep.tile([P, U], F32, name=f"lift{t}")
+                for cols in (slice(0, U // 2), slice(U // 2, U)):
+                    nc.gpsimd.tensor_tensor(gap[:, cols], other[t][:, cols], score[t][:, cols], SUB)
+                    nc.scalar.activation(lift[:, cols], gap[:, cols], RELU)
+                    nc.gpsimd.tensor_tensor(best[t][:, cols], lift[:, cols], score[t][:, cols], ADD)
+        for t in range(2, PACK):
+            for first, w in runs(t):
+                nc.vector.scalar_tensor_tensor(
+                    best[t][:, first : first + w], s_sum(t, first, w), 0.0625, other[t][:, first : first + w], MULT, MAX
+                )
+        for t in (2, 3, 0, 1):
+            for first, w in runs(t):
+                nc.scalar.activation(less_half[t][:, first : first + w], s_sum(t, first, w), COPY, scale=-0.03125)
 
         out_rows = out_0.rearrange("(p t) w -> p t w", t=PACK)
         out_words = words_of(out_1)
@@ -210,22 +246,29 @@ def tile_picked_pqcpagezhopb_none_po_kernel(
             nc.sync.dma_start(out_words[:, first : first + w], y_words[:].bitcast(I32))
 
         for i, (first, w) in enumerate(OUT_PIECES):
+            last = i + 1 == len(OUT_PIECES)
             y = keep.tile([P, PACK, w], F32, name=f"y{i}")
-            for t in range(PACK):
-                nc.vector.tensor_tensor(
-                    y[:, t, :],
-                    best[t][:].indirect(entries(n4_sb, first, w)),
-                    less_half[t][:, first : first + w],
-                    ADD,
-                )
-            nc.sync.dma_start(out_rows[:, :, first : first + w], y[:])
             rounded.append(keep.tile([P, w, PACK], BF16, name=f"y_round{i}", align_bytes=64))
-            if i + 1 < len(OUT_PIECES):
+            for pair in (slice(2, 4), slice(0, 2)):
+                for t in range(pair.start, pair.stop):
+                    nc.vector.tensor_tensor(
+                        y[:, t, :],
+                        best[t][:].indirect(entries(n4_sb, first, w)),
+                        less_half[t][:, first : first + w],
+                        ADD,
+                    )
+                if last:
+                    nc.sync.dma_start(out_rows[:, pair, first : first + w], y[:, pair, :])
+                    turned = y[:, pair, :].rearrange("p t w -> p w t")
+                    if pair.start == 2:
+                        nc.scalar.copy(rounded[i][:, :, pair], turned)
+                    else:
+                        nc.vector.tensor_copy(rounded[i][:, :, pair], turned)
+            if not last:
+                nc.sync.dma_start(out_rows[:, :, first : first + w], y[:])
                 nc.scalar.copy(rounded[i][:], y[:].rearrange("p t w -> p w t"))
-            else:
-                nc.vector.tensor_copy(rounded[i][:], y[:].rearrange("p t w -> p w t"))
             if i > 0:
                 finish(i - 1)
         finish(len(OUT_PIECES) - 1)
         for j in range(4):
-            nc.scalar.dma_start(out_2[0][j:16:4, :].bitcast(I32), y_scales[j:P:32, :].bitcast(I32))
+            (nc.scalar if j < 3 else nc.sync).dma_start(out_2[0][j:16:4, :].bitcast(I32), y_scales[j:P:32, :].bitcast(I32))

@@ -48,8 +48,10 @@ def tile_picked_pqcpagezhopb_none_po_kernel(
         def words_of(planes):
             return planes[0].rearrange("p n t -> p (n t)").bitcast(I32)
 
-        def deal(dst, src):
-            nc.vector.tensor_copy(dst.rearrange("p (t m) -> p t m", t=PACK), src.rearrange("p (m t) -> p t m", t=PACK))
+        def deal(dst, src, tiles=slice(0, PACK)):
+            run = 16 if src.dtype == U8 else 4
+            by_tile = src.rearrange("p (b m t) -> p b t m", t=PACK, m=run)
+            nc.vector.tensor_copy(dst.rearrange("p (t b m) -> p b t m", b=P // run, m=run), by_tile[:, :, tiles, :])
 
         d_scale_table = keep.tile([P, G], U8, align_bytes=64)
         x_scale_table = keep.tile([P, T], U8, align_bytes=64)
@@ -60,11 +62,11 @@ def tile_picked_pqcpagezhopb_none_po_kernel(
         k1_sb = load_list(k1, "k1_sb")
         x_table = keep.tile([P, T], U32, align_bytes=64)
         nc.sync.dma_start(x_table[:].bitcast(I32), words_of(x_words))
-        nc.scalar.dma_start(d_scale_table[0:P:8, :].bitcast(I32), d_scales[0].bitcast(I32))
+        nc.sync.dma_start(d_scale_table[0:P:8, :].bitcast(I32), d_scales[0].bitcast(I32))
         offs_sb = load_list(offs, "offs_sb")
         n2_sb = load_list(n2, "n2_sb")
         n1_sb = load_list(n1, "n1_sb")
-        d_table = keep.tile([P, G], U32, align_bytes=64)
+        d_table = keep.tile([P, G], U32, align_bytes=64, tag="d_table")
         nc.sync.dma_start(d_table[:].bitcast(I32), words_of(d_words))
         for j in range(4):
             nc.sync.dma_start(x_scale_table[j:P:32, :].bitcast(I32), x_scales[0][j:16:4, :].bitcast(I32))
@@ -92,10 +94,10 @@ def tile_picked_pqcpagezhopb_none_po_kernel(
 
         xq_words = keep.tile([P, S], U32, align_bytes=64)
         nc.vector.tensor_copy(xq_words[:], x_table[:].indirect(offs_sb[:]))
-        xq_scales = keep.tile([P, S], U8, align_bytes=64)
-        nc.vector.tensor_copy(xq_scales[:], x_scale_table[:].indirect(offs_sb[:]))
         d_picked = keep.tile([P, H], U32, align_bytes=64, tag="picked")
         nc.vector.tensor_copy(d_picked[:], d_table[:].indirect(k1_sb[:]))
+        xq_scales = keep.tile([P, S], U8, align_bytes=64)
+        nc.vector.tensor_copy(xq_scales[:], x_scale_table[:].indirect(offs_sb[:]))
         d_dealt = keep.tile([P, H], U32, align_bytes=64)
         deal(d_dealt[:].bitcast(I32), d_picked[:].bitcast(I32))
 
@@ -124,17 +126,17 @@ def tile_picked_pqcpagezhopb_none_po_kernel(
             nc.scalar.activation(cut[t][:, :S], positive[:], COPY, scale=gain_neg[:, t : t + 1])
             nc.scalar.activation(whole[t], h_sum[:], COPY, scale=gain_pos[:, t : t + 1])
 
-        c_picked = keep.tile([P, C], U32, align_bytes=64, tag="picked")
+        c_picked = keep.tile([P, C], U32, align_bytes=64, tag="d_table")
         nc.vector.tensor_copy(c_picked[:], x_table[:].indirect(cand_sb[:]))
-        c_dealt = keep.tile([P, C], U32, align_bytes=64)
-        deal(c_dealt[:].bitcast(I32), c_picked[:].bitcast(I32))
+        c_first = keep.tile([P, P], U32, align_bytes=64)
+        deal(c_first[:].bitcast(I32), c_picked[:].bitcast(I32), slice(0, 1))
 
         c_scale_picked = keep.tile([P, C], U8, align_bytes=64, tag="picked")
         nc.vector.tensor_copy(c_scale_picked[:], x_scale_table[:].indirect(cand_sb[:]))
-        c_scale_dealt = keep.tile([P, C], U8, align_bytes=64)
-        deal(c_scale_dealt[:], c_scale_picked[:])
+        c_scale_first = keep.tile([P, P], U8, align_bytes=64)
+        deal(c_scale_first[:], c_scale_picked[:], slice(0, 1))
 
-        z_round = [keep.tile([P, w, PACK], BF16, name=f"z_round{i}", align_bytes=64) for i, (c0, w) in enumerate(Z_PIECES)]
+        z_round = [keep.tile([P, w, PACK], BF16, name=f"z_round{i}", tag=f"z_round{i}", align_bytes=64) for i, (c0, w) in enumerate(Z_PIECES)]
         fetched = [keep.tile([P, S], F32, name=f"fetched{t}") for t in range(PACK)]
 
         def fetch_cut(t):
@@ -167,6 +169,11 @@ def tile_picked_pqcpagezhopb_none_po_kernel(
                 in_=z_round[i][:].rearrange("p w t -> p (w t)"),
             )
 
+        c_rest = keep.tile([P, C - P], U32, tag="z_round1", align_bytes=64)
+        deal(c_rest[:].bitcast(I32), c_picked[:].bitcast(I32), slice(1, PACK))
+        c_scale_rest = keep.tile([P, C - P], U8, tag="z_round3", align_bytes=64)
+        deal(c_scale_rest[:], c_scale_picked[:], slice(1, PACK))
+
         banks = [psum.tile([P, 512], F32, name=f"s_sum{b}", tag=f"bank{b}") for b in range(8)]
 
         def s_sum(t, first, w):
@@ -185,11 +192,11 @@ def tile_picked_pqcpagezhopb_none_po_kernel(
 
         def multiply(t, i):
             first, w = Z_PIECES[i]
-            rows = slice(t * P, (t + 1) * P)
+            rows = slice((t - 1) * P, t * P)
             nc.tensor.matmul_mx(
                 out=s_sum(t, first, w),
-                lhsT=c_dealt[:, rows].bitcast(FP8X4),
-                lhsT_scale=c_scale_dealt[:, rows],
+                lhsT=(c_rest[:, rows] if t else c_first[:]).bitcast(FP8X4),
+                lhsT_scale=c_scale_rest[:, rows] if t else c_scale_first[:],
                 rhs=z_words[i][:].bitcast(FP8X4),
                 rhs_scale=z_scales[i][:],
                 start=True,

@@ -22,7 +22,17 @@ RELU = mybir.ActivationFunctionType.Relu
 P = 128
 PACK = 4
 STRIPE = 16
-Z_PIECES = ((0, 256), (256, 256), (512, 256), (768, 256))
+QUADRANT = 32
+SCALE_ROWS = 16
+LINE = 16
+BANK = 512
+BANKS = 8
+SIXTEENTH = 0.0625
+
+Z_WIDTH = 256
+Z_ON_VECTOR = 2
+Z_ORDER = (2, 0, 1, 3)
+MAX_ON_GPSIMD = 2
 OUT_PIECES = ((0, 512), (512, 256), (768, 256))
 
 
@@ -45,11 +55,11 @@ def tile_picked_pqcpagezhopb_none_po_kernel(
         def entries(held, first, count):
             return held[:, first // STRIPE : (first + count) // STRIPE]
 
-        def words_of(planes):
-            return planes[0].rearrange("p n t -> p (n t)").bitcast(I32)
+        def words_of(codes):
+            return codes[0].rearrange("p n t -> p (n t)").bitcast(I32)
 
         def deal(dst, src, tiles=slice(0, PACK)):
-            run = 16 if src.dtype == U8 else 4
+            run = LINE if src.dtype == U8 else LINE // 4
             by_tile = src.rearrange("p (b m t) -> p b t m", t=PACK, m=run)
             nc.vector.tensor_copy(dst.rearrange("p (t b m) -> p b t m", b=P // run, m=run), by_tile[:, :, tiles, :])
 
@@ -62,14 +72,14 @@ def tile_picked_pqcpagezhopb_none_po_kernel(
         k1_sb = load_list(k1, "k1_sb")
         x_table = keep.tile([P, T], U32, align_bytes=64)
         nc.sync.dma_start(x_table[:].bitcast(I32), words_of(x_words))
-        nc.sync.dma_start(d_scale_table[0:P:8, :].bitcast(I32), d_scales[0].bitcast(I32))
+        nc.sync.dma_start(d_scale_table[0 : P : P // SCALE_ROWS, :].bitcast(I32), d_scales[0].bitcast(I32))
         offs_sb = load_list(offs, "offs_sb")
         n2_sb = load_list(n2, "n2_sb")
         n1_sb = load_list(n1, "n1_sb")
         d_table = keep.tile([P, G], U32, align_bytes=64, tag="d_table")
         nc.sync.dma_start(d_table[:].bitcast(I32), words_of(d_words))
         for j in range(4):
-            nc.sync.dma_start(x_scale_table[j:P:32, :].bitcast(I32), x_scales[0][j:16:4, :].bitcast(I32))
+            nc.sync.dma_start(x_scale_table[j:P:QUADRANT, :].bitcast(I32), x_scales[0][j:SCALE_ROWS:4, :].bitcast(I32))
         gain = keep.tile([P, PACK], F32)
         nc.gpsimd.dma_start(gain[:], gs.rearrange("(p t) o -> p (t o)", t=PACK))
         cand_sb = load_list(cand, "cand_sb")
@@ -78,19 +88,21 @@ def tile_picked_pqcpagezhopb_none_po_kernel(
 
         pages = [keep.tile([P, U], F32, name=f"page{t}") for t in range(PACK)]
         for t in range(PACK):
-            (nc.vector if t < 2 else nc.gpsimd).memset(pages[t][:].bitcast(I32), 0)
+            (nc.vector if t < PACK // 2 else nc.gpsimd).memset(pages[t][:].bitcast(I32), 0)
 
         gain_pos = keep.tile([P, PACK], F32)
         gain_neg = keep.tile([P, PACK], F32)
-        nc.scalar.activation(gain_pos[:], gain[:], COPY, scale=0.0625)
-        nc.scalar.activation(gain_neg[:], gain[:], COPY, scale=-0.0625)
+        nc.scalar.activation(gain_pos[:], gain[:], COPY, scale=SIXTEENTH)
+        nc.scalar.activation(gain_neg[:], gain[:], COPY, scale=-SIXTEENTH)
 
         d_scale_picked = keep.tile([P, H], U8, align_bytes=64)
         nc.vector.tensor_copy(d_scale_picked[:], d_scale_table[:].indirect(k1_sb[:]))
         d_scale_placed = keep.tile([P, H], U8, align_bytes=64)
         deal(d_scale_placed[:], d_scale_picked[:])
         for j in range(1, 4):
-            nc.scalar.dma_start(d_scale_placed[j:P:32, :].bitcast(I32), d_scale_placed[8 * j : P : 32, :].bitcast(I32))
+            nc.scalar.dma_start(
+                d_scale_placed[j:P:QUADRANT, :].bitcast(I32), d_scale_placed[8 * j : P : QUADRANT, :].bitcast(I32)
+            )
 
         xq_words = keep.tile([P, S], U32, align_bytes=64)
         nc.vector.tensor_copy(xq_words[:], x_table[:].indirect(offs_sb[:]))
@@ -101,7 +113,7 @@ def tile_picked_pqcpagezhopb_none_po_kernel(
         d_dealt = keep.tile([P, H], U32, align_bytes=64)
         deal(d_dealt[:].bitcast(I32), d_picked[:].bitcast(I32))
 
-        cut, whole = [], []
+        parts = []
         for t in range(PACK):
             rows = slice(t * P, (t + 1) * P)
             h_sum = psum.tile([P, S], F32, name=f"h_sum{t}", tag=f"bank{t}")
@@ -116,85 +128,74 @@ def tile_picked_pqcpagezhopb_none_po_kernel(
             )
             positive = ring.tile([P, S], F32, name="positive")
             nc.scalar.activation(positive[:], h_sum[:], RELU)
-            if t == 0:
-                cut.append(keep.tile([P, S], F32, name="cut0"))
-                whole0 = keep.tile([P, S], F32)
-                whole.append(whole0[:])
-            else:
-                cut.append(keep.tile([P, 2 * S], F32, name=f"cut{t}"))
-                whole.append(cut[t][:, S:])
-            nc.scalar.activation(cut[t][:, :S], positive[:], COPY, scale=gain_neg[:, t : t + 1])
-            nc.scalar.activation(whole[t], h_sum[:], COPY, scale=gain_pos[:, t : t + 1])
+            parts.append(keep.tile([P, 2 * S], F32, name=f"parts{t}"))
+            nc.scalar.activation(parts[t][:, :S], positive[:], COPY, scale=gain_neg[:, t : t + 1])
+            nc.scalar.activation(parts[t][:, S:], h_sum[:], COPY, scale=gain_pos[:, t : t + 1])
 
         c_picked = keep.tile([P, C], U32, align_bytes=64, tag="d_table")
         nc.vector.tensor_copy(c_picked[:], x_table[:].indirect(cand_sb[:]))
         c_first = keep.tile([P, P], U32, align_bytes=64)
         deal(c_first[:].bitcast(I32), c_picked[:].bitcast(I32), slice(0, 1))
-
         c_scale_picked = keep.tile([P, C], U8, align_bytes=64, tag="picked")
         nc.vector.tensor_copy(c_scale_picked[:], x_scale_table[:].indirect(cand_sb[:]))
         c_scale_first = keep.tile([P, P], U8, align_bytes=64)
         deal(c_scale_first[:], c_scale_picked[:], slice(0, 1))
 
-        z_round = [keep.tile([P, w, PACK], BF16, name=f"z_round{i}", tag=f"z_round{i}", align_bytes=64) for i, (c0, w) in enumerate(Z_PIECES)]
+        z_round = [
+            keep.tile([P, Z_WIDTH, PACK], BF16, name=f"z_round{i}", tag=f"z_round{i}", align_bytes=64)
+            for i in range(U // Z_WIDTH)
+        ]
         fetched = [keep.tile([P, S], F32, name=f"fetched{t}") for t in range(PACK)]
 
-        def fetch_cut(t):
-            count = cut[t].shape[1] // 2
-            for first in range(0, S, count):
-                nc.vector.tensor_copy(fetched[t][:, first : first + count], cut[t][:].indirect(entries(n2_sb, first, count)))
+        def fetch_by_n2(t):
+            nc.vector.tensor_copy(fetched[t][:], parts[t][:].indirect(n2_sb[:]))
 
-        fetch_cut(0)
+        fetch_by_n2(0)
         for t in range(PACK):
             if t + 1 < PACK:
-                fetch_cut(t + 1)
-            nc.vector.tensor_tensor(pages[t][:].indirect(n1_sb[:]), fetched[t][:], whole[t], ADD)
-            for i, (first, w) in enumerate(Z_PIECES):
-                if t == PACK - 1 and i < 2:
-                    nc.vector.tensor_copy(z_round[i][:, :, t], pages[t][:, first : first + w])
-                elif t == PACK - 2 and i < 2:
-                    both = pages[t][:, first : first + w].unsqueeze(2).to_broadcast([P, w, 2])
-                    nc.scalar.copy(z_round[i][:, :, t:], both)
+                fetch_by_n2(t + 1)
+            nc.vector.tensor_tensor(pages[t][:].indirect(n1_sb[:]), fetched[t][:], parts[t][:, S:], ADD)
+            for i in range(U // Z_WIDTH):
+                values = pages[t][:, i * Z_WIDTH : (i + 1) * Z_WIDTH]
+                if t == PACK - 1 and i < Z_ON_VECTOR:
+                    nc.vector.tensor_copy(z_round[i][:, :, t], values)
+                elif t == PACK - 2 and i < Z_ON_VECTOR:
+                    nc.scalar.copy(z_round[i][:, :, t:], values.unsqueeze(2).to_broadcast([P, Z_WIDTH, 2]))
                 else:
-                    nc.scalar.copy(z_round[i][:, :, t], pages[t][:, first : first + w])
+                    nc.scalar.copy(z_round[i][:, :, t], values)
 
         z_words, z_scales = {}, {}
-        for i in (2, 0, 1, 3):
-            w = Z_PIECES[i][1]
-            z_words[i] = keep.tile([P, w], U32, name=f"z_words{i}", align_bytes=64)
-            z_scales[i] = keep.tile([P, w], U8, name=f"z_scales{i}", align_bytes=64)
+        for i in Z_ORDER:
+            z_words[i] = keep.tile([P, Z_WIDTH], U32, name=f"z_words{i}", align_bytes=64)
+            z_scales[i] = keep.tile([P, Z_WIDTH], U8, name=f"z_scales{i}", align_bytes=64)
             nc.vector.quantize_mx(
                 out=z_words[i][:].bitcast(FP8X4),
                 scales=z_scales[i][:],
                 in_=z_round[i][:].rearrange("p w t -> p (w t)"),
             )
 
-        c_rest = keep.tile([P, C - P], U32, tag="z_round1", align_bytes=64)
+        c_rest = keep.tile([P, C - P], U32, tag=f"z_round{Z_ORDER[-2]}", align_bytes=64)
         deal(c_rest[:].bitcast(I32), c_picked[:].bitcast(I32), slice(1, PACK))
-        c_scale_rest = keep.tile([P, C - P], U8, tag="z_round3", align_bytes=64)
+        c_scale_rest = keep.tile([P, C - P], U8, tag=f"z_round{Z_ORDER[-1]}", align_bytes=64)
         deal(c_scale_rest[:], c_scale_picked[:], slice(1, PACK))
 
-        banks = [psum.tile([P, 512], F32, name=f"s_sum{b}", tag=f"bank{b}") for b in range(8)]
+        banks = [psum.tile([P, BANK], F32, name=f"s_sum{b}", tag=f"bank{b}") for b in range(BANKS)]
+        half_banked = (0, PACK - 1)
 
-        def s_sum(t, first, w):
-            if t in (0, 3):
-                return banks[first // 256][:, (t // 3) * 256 : (t // 3) * 256 + w]
-            return banks[2 + 2 * t + first // 512][:, first % 512 : first % 512 + w]
+        def s_sum(t, first, width):
+            if t in half_banked:
+                start = half_banked.index(t) * Z_WIDTH
+                return banks[first // Z_WIDTH][:, start : start + width]
+            return banks[2 + 2 * t + first // BANK][:, first % BANK : first % BANK + width]
 
-        def runs(t):
-            w = 256 if t in (0, 3) else 512
-            return [(first, w) for first in range(0, U, w)]
-
-        score = [keep.tile([P, U], F32, name=f"score{t}") for t in range(PACK)]
-        less_half = [keep.tile([P, U], F32, name=f"less_half{t}") for t in range(PACK)]
-        best = [keep.tile([P, U], F32, name=f"best{t}") for t in range(PACK)]
-        other = [keep.tile([P, U], F32, name=f"other{t}") for t in range(PACK)]
+        def bank_runs(t):
+            width = Z_WIDTH if t in half_banked else BANK
+            return [(first, width) for first in range(0, U, width)]
 
         def multiply(t, i):
-            first, w = Z_PIECES[i]
             rows = slice((t - 1) * P, t * P)
             nc.tensor.matmul_mx(
-                out=s_sum(t, first, w),
+                out=s_sum(t, i * Z_WIDTH, Z_WIDTH),
                 lhsT=(c_rest[:, rows] if t else c_first[:]).bitcast(FP8X4),
                 lhsT_scale=c_scale_rest[:, rows] if t else c_scale_first[:],
                 rhs=z_words[i][:].bitcast(FP8X4),
@@ -203,79 +204,85 @@ def tile_picked_pqcpagezhopb_none_po_kernel(
                 stop=True,
             )
 
-        for i in (2, 0, 1, 3):
+        score = [keep.tile([P, U], F32, name=f"score{t}") for t in range(PACK)]
+        less_half = [keep.tile([P, U], F32, name=f"less_half{t}") for t in range(PACK)]
+        best = [keep.tile([P, U], F32, name=f"best{t}") for t in range(PACK)]
+        other = [keep.tile([P, U], F32, name=f"other{t}") for t in range(PACK)]
+
+        def take_out(dst, t, first, width, factor):
+            nc.scalar.activation(dst[t][:, first : first + width], s_sum(t, first, width), COPY, scale=factor)
+
+        for i in Z_ORDER:
             multiply(0, i)
-            first, w = Z_PIECES[i]
-            nc.scalar.activation(score[0][:, first : first + w], s_sum(0, first, w), COPY, scale=0.0625)
+            take_out(score, 0, i * Z_WIDTH, Z_WIDTH, SIXTEENTH)
         for t in range(1, PACK):
-            for i in range(len(Z_PIECES)):
+            for i in range(U // Z_WIDTH):
                 multiply(t, i)
-            for first, w in runs(t):
-                nc.scalar.activation(score[t][:, first : first + w], s_sum(t, first, w), COPY, scale=0.0625)
+            for first, width in bank_runs(t):
+                take_out(score, t, first, width, SIXTEENTH)
 
-        def fetch_other(t):
-            for first in range(0, U, U // 2):
-                nc.vector.tensor_copy(
-                    other[t][:, first : first + U // 2], score[t][:].indirect(entries(n3_sb, first, U // 2))
-                )
-
+        halves = (slice(0, U // 2), slice(U // 2, U))
         for t in range(PACK):
-            fetch_other(t)
-            if t < 2:
-                gap = keep.tile([P, U], F32, name=f"gap{t}")
+            for cols in halves:
+                nc.vector.tensor_copy(other[t][:, cols], score[t][:].indirect(entries(n3_sb, cols.start, U // 2)))
+            if t < MAX_ON_GPSIMD:
+                excess = keep.tile([P, U], F32, name=f"excess{t}")
                 lift = keep.tile([P, U], F32, name=f"lift{t}")
-                for cols in (slice(0, U // 2), slice(U // 2, U)):
-                    nc.gpsimd.tensor_tensor(gap[:, cols], other[t][:, cols], score[t][:, cols], SUB)
-                    nc.scalar.activation(lift[:, cols], gap[:, cols], RELU)
+                for cols in halves:
+                    nc.gpsimd.tensor_tensor(excess[:, cols], other[t][:, cols], score[t][:, cols], SUB)
+                    nc.scalar.activation(lift[:, cols], excess[:, cols], RELU)
                     nc.gpsimd.tensor_tensor(best[t][:, cols], lift[:, cols], score[t][:, cols], ADD)
-        for t in range(2, PACK):
-            for first, w in runs(t):
+        for t in range(MAX_ON_GPSIMD, PACK):
+            for first, width in bank_runs(t):
+                cols = slice(first, first + width)
                 nc.vector.scalar_tensor_tensor(
-                    best[t][:, first : first + w], s_sum(t, first, w), 0.0625, other[t][:, first : first + w], MULT, MAX
+                    best[t][:, cols], s_sum(t, first, width), SIXTEENTH, other[t][:, cols], MULT, MAX
                 )
-        for t in (2, 3, 0, 1):
-            for first, w in runs(t):
-                nc.scalar.activation(less_half[t][:, first : first + w], s_sum(t, first, w), COPY, scale=-0.03125)
+
+        pairs = (slice(2, 4), slice(0, 2))
+        for pair in pairs:
+            for t in range(pair.start, pair.stop):
+                for first, width in bank_runs(t):
+                    take_out(less_half, t, first, width, -SIXTEENTH / 2)
 
         out_rows = out_0.rearrange("(p t) w -> p t w", t=PACK)
         out_words = words_of(out_1)
         y_scales = keep.tile([P, U], U8, align_bytes=64)
-        rounded = []
+        y_round = []
 
-        def finish(i):
-            first, w = OUT_PIECES[i]
-            y_words = keep.tile([P, w], U32, name=f"y_words{i}", align_bytes=64)
+        def quantise_out(i):
+            first, width = OUT_PIECES[i]
+            y_words = keep.tile([P, width], U32, name=f"y_words{i}", align_bytes=64)
             nc.vector.quantize_mx(
                 out=y_words[:].bitcast(FP8X4),
-                scales=y_scales[:, first : first + w],
-                in_=rounded[i][:].rearrange("p w t -> p (w t)"),
+                scales=y_scales[:, first : first + width],
+                in_=y_round[i][:].rearrange("p w t -> p (w t)"),
             )
-            nc.sync.dma_start(out_words[:, first : first + w], y_words[:].bitcast(I32))
+            nc.sync.dma_start(out_words[:, first : first + width], y_words[:].bitcast(I32))
 
-        for i, (first, w) in enumerate(OUT_PIECES):
+        for i, (first, width) in enumerate(OUT_PIECES):
             last = i + 1 == len(OUT_PIECES)
-            y = keep.tile([P, PACK, w], F32, name=f"y{i}")
-            rounded.append(keep.tile([P, w, PACK], BF16, name=f"y_round{i}", align_bytes=64))
-            for pair in (slice(2, 4), slice(0, 2)):
+            cols = slice(first, first + width)
+            y = keep.tile([P, PACK, width], F32, name=f"y{i}")
+            y_round.append(keep.tile([P, width, PACK], BF16, name=f"y_round{i}", align_bytes=64))
+            for pair in pairs:
                 for t in range(pair.start, pair.stop):
                     nc.vector.tensor_tensor(
-                        y[:, t, :],
-                        best[t][:].indirect(entries(n4_sb, first, w)),
-                        less_half[t][:, first : first + w],
-                        ADD,
+                        y[:, t, :], best[t][:].indirect(entries(n4_sb, first, width)), less_half[t][:, cols], ADD
                     )
                 if last:
-                    nc.sync.dma_start(out_rows[:, pair, first : first + w], y[:, pair, :])
+                    nc.sync.dma_start(out_rows[:, pair, cols], y[:, pair, :])
                     turned = y[:, pair, :].rearrange("p t w -> p w t")
-                    if pair.start == 2:
-                        nc.scalar.copy(rounded[i][:, :, pair], turned)
+                    if pair == pairs[0]:
+                        nc.scalar.copy(y_round[i][:, :, pair], turned)
                     else:
-                        nc.vector.tensor_copy(rounded[i][:, :, pair], turned)
+                        nc.vector.tensor_copy(y_round[i][:, :, pair], turned)
             if not last:
-                nc.sync.dma_start(out_rows[:, :, first : first + w], y[:])
-                nc.scalar.copy(rounded[i][:], y[:].rearrange("p t w -> p w t"))
+                nc.sync.dma_start(out_rows[:, :, cols], y[:])
+                nc.scalar.copy(y_round[i][:], y[:].rearrange("p t w -> p w t"))
             if i > 0:
-                finish(i - 1)
-        finish(len(OUT_PIECES) - 1)
+                quantise_out(i - 1)
+        quantise_out(len(OUT_PIECES) - 1)
         for j in range(4):
-            (nc.scalar if j < 3 else nc.sync).dma_start(out_2[0][j:16:4, :].bitcast(I32), y_scales[j:P:32, :].bitcast(I32))
+            queue = nc.scalar if j < 3 else nc.sync
+            queue.dma_start(out_2[0][j:SCALE_ROWS:4, :].bitcast(I32), y_scales[j:P:QUADRANT, :].bitcast(I32))

from contextlib import ExitStack

import concourse.mybir as mybir

K, T, S, G, H, U, C = 512, 1024, 512, 2048, 512, 1024, 512
FLOPS = 2 * K * H * S + 2 * H * C * U

F32 = mybir.dt.float32
BF16 = mybir.dt.bfloat16
I32 = mybir.dt.int32
U32 = mybir.dt.uint32
U16 = mybir.dt.uint16
U8 = mybir.dt.uint8
FP8X4 = mybir.dt.float8_e4m3fn_x4
ADD = mybir.AluOpType.add
MAX = mybir.AluOpType.max
MULT = mybir.AluOpType.mult
SUB = mybir.AluOpType.subtract
COPY = mybir.ActivationFunctionType.Copy
RELU = mybir.ActivationFunctionType.Relu

P = 128
PACK = 4
STRIPE = 16
QUADRANT = 32
SCALE_ROWS = 16
LINE = 16
BANK = 512
BANKS = 8
SIXTEENTH = 0.0625

Z_WIDTH = 256
Z_ON_VECTOR = 2
Z_ORDER = (2, 0, 1, 3)
MAX_ON_GPSIMD = 2
OUT_PIECES = ((0, 512), (512, 256), (768, 256))


def tile_picked_pqcpagezhopb_none_po_kernel(
    tc, x_words, x_scales, d_words, d_scales, gs, offs, k1, n1, n2, cand, n3, n4, out_0, out_1, out_2
):
    nc = tc.nc

    with ExitStack() as ctx:
        lists = ctx.enter_context(tc.tile_pool(name="lists", bufs=1))
        keep = ctx.enter_context(tc.tile_pool(name="keep", bufs=1))
        ring = ctx.enter_context(tc.tile_pool(name="ring", bufs=2))
        psum = ctx.enter_context(tc.psum_pool(name="psum", bufs=1))

        def load_list(src, name):
            held = lists.tile(list(src.shape), U16, name=name)
            nc.sync.dma_start(held[:], src)
            return held

        def entries(held, first, count):
            return held[:, first // STRIPE : (first + count) // STRIPE]

        def words_of(codes):
            return codes[0].rearrange("p n t -> p (n t)").bitcast(I32)

        def deal(dst, src, tiles=slice(0, PACK)):
            run = LINE if src.dtype == U8 else LINE // 4
            by_tile = src.rearrange("p (b m t) -> p b t m", t=PACK, m=run)
            nc.vector.tensor_copy(dst.rearrange("p (t b m) -> p b t m", b=P // run, m=run), by_tile[:, :, tiles, :])

        d_scale_table = keep.tile([P, G], U8, align_bytes=64)
        x_scale_table = keep.tile([P, T], U8, align_bytes=64)
        nc.gpsimd.memset(d_scale_table[:, : G // 2].bitcast(I32), 0)
        nc.vector.memset(d_scale_table[:, G // 2 :].bitcast(I32), 0)
        nc.gpsimd.memset(x_scale_table[:].bitcast(I32), 0)

        k1_sb = load_list(k1, "k1_sb")
        x_table = keep.tile([P, T], U32, align_bytes=64)
        nc.sync.dma_start(x_table[:].bitcast(I32), words_of(x_words))
        nc.sync.dma_start(d_scale_table[0 : P : P // SCALE_ROWS, :].bitcast(I32), d_scales[0].bitcast(I32))
        offs_sb = load_list(offs, "offs_sb")
        n2_sb = load_list(n2, "n2_sb")
        n1_sb = load_list(n1, "n1_sb")
        d_table = keep.tile([P, G], U32, align_bytes=64, tag="d_table")
        nc.sync.dma_start(d_table[:].bitcast(I32), words_of(d_words))
        for j in range(4):
            nc.sync.dma_start(x_scale_table[j:P:QUADRANT, :].bitcast(I32), x_scales[0][j:SCALE_ROWS:4, :].bitcast(I32))
        gain = keep.tile([P, PACK], F32)
        nc.gpsimd.dma_start(gain[:], gs.rearrange("(p t) o -> p (t o)", t=PACK))
        cand_sb = load_list(cand, "cand_sb")
        n3_sb = load_list(n3, "n3_sb")
        n4_sb = load_list(n4, "n4_sb")

        pages = [keep.tile([P, U], F32, name=f"page{t}") for t in range(PACK)]
        for t in range(PACK):
            (nc.vector if t < PACK // 2 else nc.gpsimd).memset(pages[t][:].bitcast(I32), 0)

        gain_pos = keep.tile([P, PACK], F32)
        gain_neg = keep.tile([P, PACK], F32)
        nc.scalar.activation(gain_pos[:], gain[:], COPY, scale=SIXTEENTH)
        nc.scalar.activation(gain_neg[:], gain[:], COPY, scale=-SIXTEENTH)

        d_scale_picked = keep.tile([P, H], U8, align_bytes=64)
        nc.vector.tensor_copy(d_scale_picked[:], d_scale_table[:].indirect(k1_sb[:]))
        d_scale_placed = keep.tile([P, H], U8, align_bytes=64)
        deal(d_scale_placed[:], d_scale_picked[:])
        for j in range(1, 4):
            nc.scalar.dma_start(
                d_scale_placed[j:P:QUADRANT, :].bitcast(I32), d_scale_placed[8 * j : P : QUADRANT, :].bitcast(I32)
            )

        xq_words = keep.tile([P, S], U32, align_bytes=64)
        nc.vector.tensor_copy(xq_words[:], x_table[:].indirect(offs_sb[:]))
        d_picked = keep.tile([P, H], U32, align_bytes=64, tag="picked")
        nc.vector.tensor_copy(d_picked[:], d_table[:].indirect(k1_sb[:]))
        xq_scales = keep.tile([P, S], U8, align_bytes=64)
        nc.vector.tensor_copy(xq_scales[:], x_scale_table[:].indirect(offs_sb[:]))
        d_dealt = keep.tile([P, H], U32, align_bytes=64)
        deal(d_dealt[:].bitcast(I32), d_picked[:].bitcast(I32))

        parts = []
        for t in range(PACK):
            rows = slice(t * P, (t + 1) * P)
            h_sum = psum.tile([P, S], F32, name=f"h_sum{t}", tag=f"bank{t}")
            nc.tensor.matmul_mx(
                out=h_sum[:],
                lhsT=d_dealt[:, rows].bitcast(FP8X4),
                lhsT_scale=d_scale_placed[:, rows],
                rhs=xq_words[:].bitcast(FP8X4),
                rhs_scale=xq_scales[:],
                start=True,
                stop=True,
            )
            positive = ring.tile([P, S], F32, name="positive")
            nc.scalar.activation(positive[:], h_sum[:], RELU)
            parts.append(keep.tile([P, 2 * S], F32, name=f"parts{t}"))
            nc.scalar.activation(parts[t][:, :S], positive[:], COPY, scale=gain_neg[:, t : t + 1])
            nc.scalar.activation(parts[t][:, S:], h_sum[:], COPY, scale=gain_pos[:, t : t + 1])

        c_picked = keep.tile([P, C], U32, align_bytes=64, tag="d_table")
        nc.vector.tensor_copy(c_picked[:], x_table[:].indirect(cand_sb[:]))
        c_first = keep.tile([P, P], U32, align_bytes=64)
        deal(c_first[:].bitcast(I32), c_picked[:].bitcast(I32), slice(0, 1))
        c_scale_picked = keep.tile([P, C], U8, align_bytes=64, tag="picked")
        nc.vector.tensor_copy(c_scale_picked[:], x_scale_table[:].indirect(cand_sb[:]))
        c_scale_first = keep.tile([P, P], U8, align_bytes=64)
        deal(c_scale_first[:], c_scale_picked[:], slice(0, 1))

        z_round = [
            keep.tile([P, Z_WIDTH, PACK], BF16, name=f"z_round{i}", tag=f"z_round{i}", align_bytes=64)
            for i in range(U // Z_WIDTH)
        ]
        fetched = [keep.tile([P, S], F32, name=f"fetched{t}") for t in range(PACK)]

        def fetch_by_n2(t):
            nc.vector.tensor_copy(fetched[t][:], parts[t][:].indirect(n2_sb[:]))

        fetch_by_n2(0)
        for t in range(PACK):
            if t + 1 < PACK:
                fetch_by_n2(t + 1)
            nc.vector.tensor_tensor(pages[t][:].indirect(n1_sb[:]), fetched[t][:], parts[t][:, S:], ADD)
            for i in range(U // Z_WIDTH):
                values = pages[t][:, i * Z_WIDTH : (i + 1) * Z_WIDTH]
                if t == PACK - 1 and i < Z_ON_VECTOR:
                    nc.vector.tensor_copy(z_round[i][:, :, t], values)
                elif t == PACK - 2 and i < Z_ON_VECTOR:
                    nc.scalar.copy(z_round[i][:, :, t:], values.unsqueeze(2).to_broadcast([P, Z_WIDTH, 2]))
                else:
                    nc.scalar.copy(z_round[i][:, :, t], values)

        z_words, z_scales = {}, {}
        for i in Z_ORDER:
            z_words[i] = keep.tile([P, Z_WIDTH], U32, name=f"z_words{i}", align_bytes=64)
            z_scales[i] = keep.tile([P, Z_WIDTH], U8, name=f"z_scales{i}", align_bytes=64)
            nc.vector.quantize_mx(
                out=z_words[i][:].bitcast(FP8X4),
                scales=z_scales[i][:],
                in_=z_round[i][:].rearrange("p w t -> p (w t)"),
            )

        c_rest = keep.tile([P, C - P], U32, tag=f"z_round{Z_ORDER[-2]}", align_bytes=64)
        deal(c_rest[:].bitcast(I32), c_picked[:].bitcast(I32), slice(1, PACK))
        c_scale_rest = keep.tile([P, C - P], U8, tag=f"z_round{Z_ORDER[-1]}", align_bytes=64)
        deal(c_scale_rest[:], c_scale_picked[:], slice(1, PACK))

        banks = [psum.tile([P, BANK], F32, name=f"s_sum{b}", tag=f"bank{b}") for b in range(BANKS)]
        half_banked = (0, PACK - 1)

        def s_sum(t, first, width):
            if t in half_banked:
                start = half_banked.index(t) * Z_WIDTH
                return banks[first // Z_WIDTH][:, start : start + width]
            return banks[2 + 2 * t + first // BANK][:, first % BANK : first % BANK + width]

        def bank_runs(t):
            width = Z_WIDTH if t in half_banked else BANK
            return [(first, width) for first in range(0, U, width)]

        def multiply(t, i):
            rows = slice((t - 1) * P, t * P)
            nc.tensor.matmul_mx(
                out=s_sum(t, i * Z_WIDTH, Z_WIDTH),
                lhsT=(c_rest[:, rows] if t else c_first[:]).bitcast(FP8X4),
                lhsT_scale=c_scale_rest[:, rows] if t else c_scale_first[:],
                rhs=z_words[i][:].bitcast(FP8X4),
                rhs_scale=z_scales[i][:],
                start=True,
                stop=True,
            )

        score = [keep.tile([P, U], F32, name=f"score{t}") for t in range(PACK)]
        less_half = [keep.tile([P, U], F32, name=f"less_half{t}") for t in range(PACK)]
        best = [keep.tile([P, U], F32, name=f"best{t}") for t in range(PACK)]
        other = [keep.tile([P, U], F32, name=f"other{t}") for t in range(PACK)]

        def take_out(dst, t, first, width, factor):
            nc.scalar.activation(dst[t][:, first : first + width], s_sum(t, first, width), COPY, scale=factor)

        for i in Z_ORDER:
            multiply(0, i)
            take_out(score, 0, i * Z_WIDTH, Z_WIDTH, SIXTEENTH)
        for t in range(1, PACK):
            for i in range(U // Z_WIDTH):
                multiply(t, i)
            for first, width in bank_runs(t):
                take_out(score, t, first, width, SIXTEENTH)

        halves = (slice(0, U // 2), slice(U // 2, U))
        for t in range(PACK):
            for cols in halves:
                nc.vector.tensor_copy(other[t][:, cols], score[t][:].indirect(entries(n3_sb, cols.start, U // 2)))
            if t < MAX_ON_GPSIMD:
                excess = keep.tile([P, U], F32, name=f"excess{t}")
                lift = keep.tile([P, U], F32, name=f"lift{t}")
                for cols in halves:
                    nc.gpsimd.tensor_tensor(excess[:, cols], other[t][:, cols], score[t][:, cols], SUB)
                    nc.scalar.activation(lift[:, cols], excess[:, cols], RELU)
                    nc.gpsimd.tensor_tensor(best[t][:, cols], lift[:, cols], score[t][:, cols], ADD)
        for t in range(MAX_ON_GPSIMD, PACK):
            for first, width in bank_runs(t):
                cols = slice(first, first + width)
                nc.vector.scalar_tensor_tensor(
                    best[t][:, cols], s_sum(t, first, width), SIXTEENTH, other[t][:, cols], MULT, MAX
                )

        pairs = (slice(2, 4), slice(0, 2))
        for pair in pairs:
            for t in range(pair.start, pair.stop):
                for first, width in bank_runs(t):
                    take_out(less_half, t, first, width, -SIXTEENTH / 2)

        out_rows = out_0.rearrange("(p t) w -> p t w", t=PACK)
        out_words = words_of(out_1)
        y_scales = keep.tile([P, U], U8, align_bytes=64)
        y_round = []

        def quantise_out(i):
            first, width = OUT_PIECES[i]
            y_words = keep.tile([P, width], U32, name=f"y_words{i}", align_bytes=64)
            nc.vector.quantize_mx(
                out=y_words[:].bitcast(FP8X4),
                scales=y_scales[:, first : first + width],
                in_=y_round[i][:].rearrange("p w t -> p (w t)"),
            )
            nc.sync.dma_start(out_words[:, first : first + width], y_words[:].bitcast(I32))

        for i, (first, width) in enumerate(OUT_PIECES):
            last = i + 1 == len(OUT_PIECES)
            cols = slice(first, first + width)
            y = keep.tile([P, PACK, width], F32, name=f"y{i}")
            y_round.append(keep.tile([P, width, PACK], BF16, name=f"y_round{i}", align_bytes=64))
            for pair in pairs:
                for t in range(pair.start, pair.stop):
                    nc.vector.tensor_tensor(
                        y[:, t, :], best[t][:].indirect(entries(n4_sb, first, width)), less_half[t][:, cols], ADD
                    )
                if last:
                    nc.sync.dma_start(out_rows[:, pair, cols], y[:, pair, :])
                    turned = y[:, pair, :].rearrange("p t w -> p w t")
                    if pair == pairs[0]:
                        nc.scalar.copy(y_round[i][:, :, pair], turned)
                    else:
                        nc.vector.tensor_copy(y_round[i][:, :, pair], turned)
            if not last:
                nc.sync.dma_start(out_rows[:, :, cols], y[:])
                nc.scalar.copy(y_round[i][:], y[:].rearrange("p t w -> p w t"))
            if i > 0:
                quantise_out(i - 1)
        quantise_out(len(OUT_PIECES) - 1)
        for j in range(4):
            queue = nc.scalar if j < 3 else nc.sync
            queue.dma_start(out_2[0][j:SCALE_ROWS:4, :].bitcast(I32), y_scales[j:P:QUADRANT, :].bitcast(I32))
